import numpy as np
import ml_dtypes


def mxq(x, axis, fmt="e4m3"):
    dtype, down = {"e4m3": (ml_dtypes.float8_e4m3fn, 7), "e5m2": (ml_dtypes.float8_e5m2, 14)}[fmt]
    v = np.moveaxis(np.asarray(x, np.float32).astype(ml_dtypes.bfloat16).astype(np.float64), axis, -1)
    blocks = v.reshape(v.shape[:-1] + (-1, 32))
    amax = np.abs(blocks).max(-1, keepdims=True)
    byte = np.maximum(np.where(amax > 0, np.frexp(amax)[1] - 1 + 127, 0) - down, 1)
    scale = np.exp2(byte - 127.0)
    codes = (blocks / scale).astype(np.float32).astype(dtype).astype(np.float64)
    return np.moveaxis((codes * scale).reshape(v.shape), -1, axis)


WIDE = False


def mx_kscale(k):
    if not WIDE:
        return np.ones(k)
    levels = np.array([10, -10, 5, -5, 0])
    if k % 512:
        return np.exp2(np.random.permutation(np.resize(levels, k // 32))).repeat(32)
    a = np.empty((k // 512, 16))
    for p in range(k // 512):
        a[p, :8] = np.random.permutation(np.resize(levels, 8))
        for g in range(8):
            far = levels[np.abs(levels - a[p, g]) >= 10]
            a[p, g + 8] = far[np.random.randint(len(far))]
    return np.exp2(a.ravel()).repeat(32)


BF16 = ml_dtypes.bfloat16


def bf(x):
    return np.asarray(x, np.float32).astype(BF16)


def f64(x):
    return np.asarray(x).astype(np.float64)


T, D, F, R = 8192, 512, 1024, 128


def draw0():
    kd, kt = mx_kscale(D), mx_kscale(T)
    return {"x": bf(np.random.standard_normal((T, D)) * kd),
            "wm": bf(np.random.standard_normal((D, F)) / np.sqrt(D) / kd[:, None]),
            "a": bf(np.random.standard_normal((D, R)) / np.sqrt(D) / kd[:, None]),
            "target": bf(np.random.standard_normal((T, F))),
            "s": bf((1.0 + 0.25 * np.random.standard_normal(T)) / kt),
            "wt": bf(np.random.uniform(0.5, 1.5, T) * kt)}


def scale_tokens(gain, rows):
    return gain[:, None] * rows


def core(x, wm, a, target, s, wt):
    root_t = np.sqrt(T)
    xq = mxq(f64(x), 1, "e4m3")
    u = xq @ mxq(f64(a), 0, "e4m3")
    y = xq @ mxq(f64(wm), 0, "e4m3")
    ug = scale_tokens(f64(s), u)
    e = scale_tokens(f64(wt), np.tanh(y - f64(target)))
    return (mxq(ug.T, 1, "e4m3") @ mxq(e, 0, "e4m3")) / root_t


def e4m3fn_bytes(y):
    return np.clip(np.asarray(y, np.float64), -448.0, 448.0).astype(np.float32).astype(ml_dtypes.float8_e4m3fn).view(np.uint8)


def e4m3fn_values(b):
    return np.asarray(b, np.uint8).view(ml_dtypes.float8_e4m3fn).astype(np.float64)


def setup_inputs():
    d = draw0()
    x0 = np.asarray(d['x']).astype(np.float64)
    s = (np.max(np.abs(x0), axis=(0,), keepdims=True) / 448.0).astype(np.float32)
    out = {}
    for k, v in d.items():
        if k == 'x':
            out['x_bytes'] = e4m3fn_bytes(x0 / s.astype(np.float64))
            out['x_scale'] = s
        else:
            out[k] = v
    return out


def reference(x_bytes, x_scale, wm, a, target, s, wt):
    return core(e4m3fn_values(x_bytes) * x_scale.astype(np.float64), wm, a, target, s, wt)

@@ -1,0 +1,295 @@
+import math
+from contextlib import ExitStack
+
+import concourse.mybir as mybir
+from concourse.masks import make_identity
+
+T, D, F, R = 8192, 512, 1024, 128
+FLOPS = 2 * T * D * (F + R) + 2 * T * R * F
+
+F32 = mybir.dt.float32
+BF16 = mybir.dt.bfloat16
+U32 = mybir.dt.uint32
+U8 = mybir.dt.uint8
+FP8 = mybir.dt.float8_e4m3fn
+FP8X4 = mybir.dt.float8_e4m3fn_x4
+ACT = mybir.ActivationFunctionType
+ALU = mybir.AluOpType
+
+P = 128
+GT = 512
+NG = T // GT
+NC = F // 128
+MAP = ["G","G","G","S","G","G","G","S"]
+
+
+def tile_lorafalogcoshgradient_t_kernel(tc, x_bytes, x_scale, wm, a, target, s, wt, out):
+    nc = tc.nc
+    with ExitStack() as ctx:
+        const = ctx.enter_context(tc.tile_pool(name="const", bufs=1))
+        load = ctx.enter_context(tc.tile_pool(name="load", bufs=4))
+        work = ctx.enter_context(tc.tile_pool(name="work", bufs=2))
+        ring = ctx.enter_context(tc.tile_pool(name="ring", bufs=6))
+        keep = ctx.enter_context(tc.tile_pool(name="keep", bufs=3))
+        ps_acc = ctx.enter_context(tc.psum_pool(name="ps_acc", bufs=1))
+        ps_xt = ctx.enter_context(tc.psum_pool(name="ps_xt", bufs=2))
+        ps_u = ctx.enter_context(tc.psum_pool(name="ps_u", bufs=1))
+        ps_y = ctx.enter_context(tc.psum_pool(name="ps_y", bufs=3))
+        ctx.enter_context(tc.manual_schedule())
+
+        st = {}
+
+        def load_x(g):
+            xby = load.tile([P, 4 * D], U8, name="xby", align_bytes=64)
+            nc.sync.dma_start(out=xby[:], in_=x_bytes[g * GT : (g + 1) * GT, :].rearrange("(p t) k -> p (t k)", t=4))
+            st["xby", g] = xby
+
+        def load_t(g, parts):
+            tg = load.tile([P, 4, F], BF16, name="tg", align_bytes=64)
+            src = target[g * GT : (g + 1) * GT, :].rearrange("(p t) f -> p t f", t=4)
+            w = F // parts
+            for i in range(parts):
+                nc.sync.dma_start(out=tg[:, :, i * w : (i + 1) * w], in_=src[:, :, i * w : (i + 1) * w])
+            st["tg", g] = tg
+
+        def cast(g, t):
+            if t == 0:
+                st["xb", g] = work.tile([P, 4 * D], BF16, name="xb", align_bytes=64)
+            nc.scalar.copy(out=st["xb", g][:, t * D : (t + 1) * D], in_=st["xby", g][:, t * D : (t + 1) * D].bitcast(FP8))
+
+        def transposes(g, pair):
+            xt = ps_xt.tile([P, 512], F32, name="xt")
+            for tt in range(2):
+                words = st["xb", g][:, (2 * pair + tt) * D : (2 * pair + tt + 1) * D].bitcast(F32)
+                for u in range(2):
+                    nc.tensor.transpose(xt[:, u * 256 + tt * 128 : u * 256 + (tt + 1) * 128], words[:, u::2], ident[:])
+            st["xt", g, pair] = xt
+
+        def scale_x(g, pair):
+            if pair == 0:
+                st["xi", g] = work.tile([P, 2048], BF16, name="xi", align_bytes=64)
+            nc.vector.tensor_tensor(
+                out=st["xi", g][:, pair * 1024 : (pair + 1) * 1024].rearrange("p (n u e) -> p n u e", u=2, e=2),
+                in0=st["xt", g, pair][:].bitcast(BF16).rearrange("p (u n e) -> p n u e", u=2, e=2),
+                in1=xsc[:].rearrange("p (u e) -> p u e", e=2).unsqueeze(1).to_broadcast([P, 256, 2, 2]),
+                op=ALU.mult,
+            )
+
+        def quant_x(g):
+            xq = work.tile([P, 512], U32, name="xq", align_bytes=64)
+            xs = work.tile([P, 512], U8, name="xs", align_bytes=64)
+            nc.vector.quantize_mx(out=xq[:].bitcast(FP8X4), scales=xs[:], in_=st["xi", g][:])
+            st["xq", g] = (xq, xs)
+
+        def mx4(bank, g, wq_, ws_, lo):
+            xq, xs = st["xq", g]
+            for t in range(4):
+                c = slice(t * 128, (t + 1) * 128)
+                nc.tensor.matmul_mx(
+                    out=bank[:, c],
+                    lhsT=xq[:, c].bitcast(FP8X4),
+                    lhsT_scale=xs[:, c],
+                    rhs=wq_[:, lo : lo + 128].bitcast(FP8X4),
+                    rhs_scale=ws_[:, lo : lo + 128],
+                    start=True,
+                    stop=True,
+                )
+
+        def mm_u(g):
+            ub = ps_u.tile([P, 512], F32, name="ub")
+            mx4(ub, g, aq, as_, 0)
+            st["ub", g] = ub
+
+        def gate_u(g):
+            ui = work.tile([P, R, 4], BF16, name="ui", align_bytes=64)
+            nc.vector.tensor_tensor(
+                out=ui[:],
+                in0=st["ub", g][:].rearrange("p (t r) -> p r t", t=4),
+                in1=sw[:, g, :].unsqueeze(1).to_broadcast([P, R, 4]),
+                op=ALU.mult,
+            )
+            st["ui", g] = ui
+
+        def quant_u(g):
+            uq = keep.tile([P, R], U32, name="uq", align_bytes=64)
+            us = keep.tile([P, R], U8, name="us", align_bytes=64)
+            nc.vector.quantize_mx(out=uq[:].bitcast(FP8X4), scales=us[:], in_=st["ui", g][:].rearrange("p r t -> p (r t)"))
+            st["uq", g] = (uq, us)
+
+        def mm_y(g, c):
+            yb = ps_y.tile([P, 512], F32, name="yb")
+            mx4(yb, g, wq, ws, c * 128)
+            st["yb", g, c] = yb
+
+        def sub(g, c):
+            z = ring.tile([P, 128, 4], F32, name="z", align_bytes=64)
+            nc.vector.tensor_tensor(
+                out=z[:],
+                in0=st["yb", g, c][:].rearrange("p (t n) -> p n t", t=4),
+                in1=st["tg", g][:, :, c * 128 : (c + 1) * 128].rearrange("p t n -> p n t"),
+                op=ALU.subtract,
+            )
+            st["z", g, c] = z
+
+        def tanh(g, c):
+            th = ring.tile([P, 128, 4], F32, name="th", align_bytes=64)
+            nc.scalar.activation(out=th[:], in_=st["z", g, c][:], func=ACT.Tanh)
+            st["th", g, c] = th
+
+        def weight(g, c):
+            h, k = divmod(c, NC // 2)
+            if k == 0:
+                st["e", g, h] = keep.tile([P, 512, 4], BF16, name="e", align_bytes=64)
+            dst = st["e", g, h][:, k * 128 : (k + 1) * 128, :]
+            th = st["th", g, c]
+            eng = MAP[c]
+            if eng == "S":
+                for t in range(4):
+                    nc.scalar.activation(out=dst[:, :, t], in_=th[:, :, t], func=ACT.Copy, scale=sw[:, NG + g, t : t + 1])
+            else:
+                (nc.gpsimd if eng == "G" else nc.vector).tensor_tensor(
+                    out=dst, in0=th[:], in1=sw[:, NG + g, :].unsqueeze(1).to_broadcast([P, 128, 4]), op=ALU.mult
+                )
+
+        def quant_e(g, h):
+            eq = keep.tile([P, 512], U32, name="eq", align_bytes=64)
+            es = keep.tile([P, 512], U8, name="es", align_bytes=64)
+            nc.vector.quantize_mx(out=eq[:].bitcast(FP8X4), scales=es[:], in_=st["e", g, h][:].rearrange("p n t -> p (n t)"))
+            st["eq", g, h] = (eq, es)
+
+        def mm_o(g, h):
+            uq, us = st["uq", g]
+            eq, es = st["eq", g, h]
+            nc.tensor.matmul_mx(
+                out=acc[h][:],
+                lhsT=uq[:].bitcast(FP8X4),
+                lhsT_scale=us[:],
+                rhs=eq[:].bitcast(FP8X4),
+                rhs_scale=es[:],
+                start=(g == 0),
+                stop=(g == NG - 1),
+            )
+
+        load_x(0)
+        xsc = const.tile([P, 4], F32, name="xsc")
+        nc.scalar.dma_start(out=xsc[:], in_=x_scale.rearrange("o (p t) -> p (o t)", t=4))
+        nat = const.tile([P, GT], BF16, name="nat")
+        nc.vector.memset(nat[:], 0.0)
+        nc.scalar.dma_start(out=nat[0:NG, :], in_=s.rearrange("(g n) -> g n", n=GT))
+        nc.scalar.dma_start(out=nat[NG : 2 * NG, :], in_=wt.rearrange("(g n) -> g n", n=GT))
+        ident = const.tile([P, P], F32, name="ident")
+        make_identity(nc, ident[:])
+        a_raw = const.tile([P, 4, R], BF16, name="a_raw")
+        nc.sync.dma_start(out=a_raw[:], in_=a.rearrange("(p j) r -> p j r", j=4))
+        w_raw = const.tile([P, 4, F], BF16, name="w_raw")
+        wsrc = wm.rearrange("(p j) f -> p j f", j=4)
+        nc.sync.dma_start(out=w_raw[:, :, 0:512], in_=wsrc[:, :, 0:512])
+        load_t(0, 2)
+        nc.sync.dma_start(out=w_raw[:, :, 512:1024], in_=wsrc[:, :, 512:1024])
+        load_x(1)
+        load_x(2)
+        load_t(1, 1)
+
+        warm = const.tile([P, 1], F32, name="warm")
+        nc.vector.memset(warm[:], 0.0)
+        nc.scalar.activation(out=warm[:], in_=warm[:], func=ACT.Tanh)
+        for t in range(4):
+            cast(0, t)
+        transposes(0, 0)
+        transposes(0, 1)
+        scale_x(0, 0)
+        scale_x(0, 1)
+        wi = const.tile([P, F, 4], BF16, name="wi", align_bytes=64)
+        ai = const.tile([P, R, 4], BF16, name="ai", align_bytes=64)
+        aq = const.tile([P, R], U32, name="aq", align_bytes=64)
+        as_ = const.tile([P, R], U8, name="as_", align_bytes=64)
+        wq = const.tile([P, F], U32, name="wq", align_bytes=64)
+        ws = const.tile([P, F], U8, name="ws", align_bytes=64)
+        nc.vector.tensor_copy(out=ai[:], in_=a_raw[:].rearrange("p j r -> p r j"))
+        quant_x(0)
+        natf = const.tile([P, GT], F32, name="natf")
+        nc.gpsimd.tensor_copy(out=natf[:], in_=nat[:])
+        nc.vector.tensor_copy(out=wi[:, 0:256, :], in_=w_raw[:, :, 0:256].rearrange("p j f -> p f j"))
+        nc.scalar.copy(out=wi[:, 256:512, :], in_=w_raw[:, :, 256:512].rearrange("p j f -> p f j"))
+        nc.vector.quantize_mx(out=aq[:].bitcast(FP8X4), scales=as_[:], in_=ai[:].rearrange("p r j -> p (r j)"))
+        sw_ps = ps_u.tile([P, 512], F32, name="ub")
+        for t in range(4):
+            nc.tensor.transpose(sw_ps[:, t * 128 : (t + 1) * 128], natf[:, t::4], ident[:])
+        sw = const.tile([P, 2 * NG, 4], F32, name="sw")
+        nc.vector.quantize_mx(out=wq[:, 0:256].bitcast(FP8X4), scales=ws[:, 0:256], in_=wi[:, 0:256, :].rearrange("p f j -> p (f j)"))
+        nc.vector.tensor_copy(out=sw[:], in_=sw_ps[:].rearrange("p (t n) -> p n t", t=4)[:, 0 : 2 * NG, :])
+        nc.vector.quantize_mx(out=wq[:, 256:512].bitcast(FP8X4), scales=ws[:, 256:512], in_=wi[:, 256:512, :].rearrange("p f j -> p (f j)"))
+        mm_u(0)
+        gate_u(0)
+        nc.vector.tensor_copy(out=wi[:, 512:768, :], in_=w_raw[:, :, 512:768].rearrange("p j f -> p f j"))
+        nc.scalar.copy(out=wi[:, 768:1024, :], in_=w_raw[:, :, 768:1024].rearrange("p j f -> p f j"))
+        quant_u(0)
+        acc = []
+        for h in range(2):
+            acc_t = ps_acc.tile([P, 512], F32, name="acc%d" % h)
+            acc.append(acc_t)
+        for t in range(4):
+            cast(1, t)
+        mm_y(0, 0)
+        mm_y(0, 1)
+        transposes(1, 0)
+        transposes(1, 1)
+
+        for i in range(NG):
+            for c in range(NC):
+                if c == 0:
+                    if i + 3 < NG:
+                        load_x(i + 3)
+                    if i + 2 < NG:
+                        load_t(i + 2, 1)
+                if c % 2 == 0 and i + 2 < NG:
+                    cast(i + 2, c // 2)
+                nxt = c + 2
+                if nxt < NC:
+                    mm_y(i, nxt)
+                elif i + 1 < NG:
+                    mm_y(i + 1, nxt - NC)
+                sub(i, c)
+                if i == 0 and c == 0:
+                    nc.vector.quantize_mx(out=wq[:, 512:768].bitcast(FP8X4), scales=ws[:, 512:768], in_=wi[:, 512:768, :].rearrange("p f j -> p (f j)"))
+                if i == 0 and c == 1:
+                    nc.vector.quantize_mx(out=wq[:, 768:1024].bitcast(FP8X4), scales=ws[:, 768:1024], in_=wi[:, 768:1024, :].rearrange("p f j -> p (f j)"))
+                tanh(i, c)
+                weight(i, c)
+                if c == 0 and i + 1 < NG:
+                    scale_x(i + 1, 0)
+                if c == 1 and i > 0:
+                    quant_e(i - 1, 1)
+                if c == 2:
+                    if i > 0:
+                        mm_o(i - 1, 0)
+                    if i + 1 < NG:
+                        scale_x(i + 1, 1)
+                if c == 3 and i > 0:
+                    mm_o(i - 1, 1)
+                if c == 4:
+                    if i + 1 < NG:
+                        quant_x(i + 1)
+                    if i + 2 < NG:
+                        transposes(i + 2, 0)
+                if c == 5 and i + 1 < NG:
+                    mm_u(i + 1)
+                if c == 6 and i + 1 < NG:
+                    gate_u(i + 1)
+                if c == 6 and i + 2 < NG:
+                    transposes(i + 2, 1)
+                if c == 7:
+                    quant_e(i, 0)
+                    if i + 1 < NG:
+                        quant_u(i + 1)
+
+        quant_e(NG - 1, 1)
+        for h in range(2):
+            mm_o(NG - 1, h)
+            res = work.tile([P, 512], F32, name="res")
+            inv = 1.0 / math.sqrt(T)
+            if h == 0:
+                nc.scalar.activation(out=res[:], in_=acc[h][:], func=ACT.Copy, scale=inv)
+            else:
+                nc.vector.tensor_scalar(out=res[:], in0=acc[h][:], scalar1=inv, scalar2=None, op0=ALU.mult)
+            nc.sync.dma_start(out=out[:, h * 512 : (h + 1) * 512], in_=res[:])

@@ -20,7 +20,10 @@ P = 128
 GT = 512
 NG = T // GT
 NC = F // 128
-MAP = ["G","G","G","S","G","G","G","S"]
+MAPS = [["S","G","G","G","S","G","G","G"],["S","G","G","G","G","G","G","G"]]
+LAST = ["S","G","S","G","V","G","V","V"]
+LAG = {"G":0,"S":1,"V":2}
+UQ = 4
 
 
 def tile_lorafalogcoshgradient_t_kernel(tc, x_bytes, x_scale, wm, a, target, s, wt, out):
@@ -31,6 +34,7 @@ def tile_lorafalogcoshgradient_t_kernel(tc, x_bytes, x_scale, wm, a, target, s, 
         work = ctx.enter_context(tc.tile_pool(name="work", bufs=2))
         ring = ctx.enter_context(tc.tile_pool(name="ring", bufs=6))
         keep = ctx.enter_context(tc.tile_pool(name="keep", bufs=3))
+        codes = ctx.enter_context(tc.tile_pool(name="codes", bufs=6))
         ps_acc = ctx.enter_context(tc.psum_pool(name="ps_acc", bufs=1))
         ps_xt = ctx.enter_context(tc.psum_pool(name="ps_xt", bufs=2))
         ps_u = ctx.enter_context(tc.psum_pool(name="ps_u", bufs=1))
@@ -52,10 +56,10 @@ def tile_lorafalogcoshgradient_t_kernel(tc, x_bytes, x_scale, wm, a, target, s, 
                 nc.sync.dma_start(out=tg[:, :, i * w : (i + 1) * w], in_=src[:, :, i * w : (i + 1) * w])
             st["tg", g] = tg
 
-        def cast(g, t):
+        def cast(g, t, n=1):
             if t == 0:
                 st["xb", g] = work.tile([P, 4 * D], BF16, name="xb", align_bytes=64)
-            nc.scalar.copy(out=st["xb", g][:, t * D : (t + 1) * D], in_=st["xby", g][:, t * D : (t + 1) * D].bitcast(FP8))
+            nc.scalar.copy(out=st["xb", g][:, t * D : (t + n) * D], in_=st["xby", g][:, t * D : (t + n) * D].bitcast(FP8))
 
         def transposes(g, pair):
             xt = ps_xt.tile([P, 512], F32, name="xt")
@@ -101,48 +105,59 @@ def tile_lorafalogcoshgradient_t_kernel(tc, x_bytes, x_scale, wm, a, target, s, 
             st["ub", g] = ub
 
         def gate_u(g):
-            ui = work.tile([P, R, 4], BF16, name="ui", align_bytes=64)
+            b, k = divmod(g, UQ)
+            if k == 0:
+                st["ui", b] = work.tile([P, UQ * R, 4], BF16, name="ui", align_bytes=64)
             nc.vector.tensor_tensor(
-                out=ui[:],
+                out=st["ui", b][:, k * R : (k + 1) * R, :],
                 in0=st["ub", g][:].rearrange("p (t r) -> p r t", t=4),
                 in1=sw[:, g, :].unsqueeze(1).to_broadcast([P, R, 4]),
                 op=ALU.mult,
             )
-            st["ui", g] = ui
 
-        def quant_u(g):
-            uq = keep.tile([P, R], U32, name="uq", align_bytes=64)
-            us = keep.tile([P, R], U8, name="us", align_bytes=64)
-            nc.vector.quantize_mx(out=uq[:].bitcast(FP8X4), scales=us[:], in_=st["ui", g][:].rearrange("p r t -> p (r t)"))
-            st["uq", g] = (uq, us)
+        def quant_u(b):
+            uq = work.tile([P, UQ * R], U32, name="uq", align_bytes=64)
+            us = work.tile([P, UQ * R], U8, name="us", align_bytes=64)
+            nc.vector.quantize_mx(out=uq[:].bitcast(FP8X4), scales=us[:], in_=st["ui", b][:].rearrange("p r t -> p (r t)"))
+            st["uq", b] = (uq, us)
 
-        def mm_y(g, c):
+        def mm_y(n):
+            g, c = divmod(n, NC)
             yb = ps_y.tile([P, 512], F32, name="yb")
             mx4(yb, g, wq, ws, c * 128)
-            st["yb", g, c] = yb
+            st["yb", n] = yb
 
-        def sub(g, c):
-            z = ring.tile([P, 128, 4], F32, name="z", align_bytes=64)
+        def sub(n):
+            g, c = divmod(n, NC)
+            z = ring.tile([P, 512], F32, name="z", align_bytes=64)
             nc.vector.tensor_tensor(
-                out=z[:],
-                in0=st["yb", g, c][:].rearrange("p (t n) -> p n t", t=4),
-                in1=st["tg", g][:, :, c * 128 : (c + 1) * 128].rearrange("p t n -> p n t"),
+                out=z[:].rearrange("p (h n t) -> p h n t", h=2, t=2),
+                in0=st["yb", n][:].rearrange("p (h t n) -> p h n t", h=2, t=2),
+                in1=st["tg", g][:, :, c * 128 : (c + 1) * 128].rearrange("p (h t) n -> p h n t", h=2),
                 op=ALU.subtract,
             )
-            st["z", g, c] = z
+            st["z", n] = z
 
-        def tanh(g, c):
+        def tanh(n):
             th = ring.tile([P, 128, 4], F32, name="th", align_bytes=64)
-            nc.scalar.activation(out=th[:], in_=st["z", g, c][:], func=ACT.Tanh)
-            st["th", g, c] = th
+            nc.scalar.activation(
+                out=th[:].rearrange("p n (h t) -> p n h t", h=2),
+                in_=st["z", n][:].rearrange("p (h n t) -> p n h t", h=2, t=2),
+                func=ACT.Tanh,
+            )
+            st["th", n] = th
 
-        def weight(g, c):
-            h, k = divmod(c, NC // 2)
-            if k == 0:
-                st["e", g, h] = keep.tile([P, 512, 4], BF16, name="e", align_bytes=64)
-            dst = st["e", g, h][:, k * 128 : (k + 1) * 128, :]
-            th = st["th", g, c]
-            eng = MAP[c]
+        def engine_of(n):
+            g, c = divmod(n, NC)
+            return LAST[c] if g == NG - 1 else MAPS[g % len(MAPS)][c]
+
+        def weight(n):
+            g, c = divmod(n, NC)
+            if ("e", g) not in st:
+                st["e", g] = keep.tile([P, F, 4], BF16, name="e", align_bytes=64)
+            dst = st["e", g][:, c * 128 : (c + 1) * 128, :]
+            th = st["th", n]
+            eng = engine_of(n)
             if eng == "S":
                 for t in range(4):
                     nc.scalar.activation(out=dst[:, :, t], in_=th[:, :, t], func=ACT.Copy, scale=sw[:, NG + g, t : t + 1])
@@ -151,141 +166,37 @@ def tile_lorafalogcoshgradient_t_kernel(tc, x_bytes, x_scale, wm, a, target, s, 
                     out=dst, in0=th[:], in1=sw[:, NG + g, :].unsqueeze(1).to_broadcast([P, 128, 4]), op=ALU.mult
                 )
 
-        def quant_e(g, h):
-            eq = keep.tile([P, 512], U32, name="eq", align_bytes=64)
-            es = keep.tile([P, 512], U8, name="es", align_bytes=64)
-            nc.vector.quantize_mx(out=eq[:].bitcast(FP8X4), scales=es[:], in_=st["e", g, h][:].rearrange("p n t -> p (n t)"))
-            st["eq", g, h] = (eq, es)
+        def quant_e(g, lo, hi):
+            if lo == 0:
+                st["eq", g] = (codes.tile([P, F], U32, name="eq", align_bytes=64), codes.tile([P, F], U8, name="es", align_bytes=64))
+            eq, es = st["eq", g]
+            nc.vector.quantize_mx(
+                out=eq[:, lo:hi].bitcast(FP8X4), scales=es[:, lo:hi], in_=st["e", g][:, lo:hi, :].rearrange("p n t -> p (n t)")
+            )
 
         def mm_o(g, h):
-            uq, us = st["uq", g]
-            eq, es = st["eq", g, h]
+            uq, us = st["uq", g // UQ]
+            eq, es = st["eq", g]
+            k = slice(g % UQ * R, (g % UQ + 1) * R)
+            f = slice(h * 512, (h + 1) * 512)
             nc.tensor.matmul_mx(
                 out=acc[h][:],
-                lhsT=uq[:].bitcast(FP8X4),
-                lhsT_scale=us[:],
-                rhs=eq[:].bitcast(FP8X4),
-                rhs_scale=es[:],
+                lhsT=uq[:, k].bitcast(FP8X4),
+                lhsT_scale=us[:, k],
+                rhs=eq[:, f].bitcast(FP8X4),
+                rhs_scale=es[:, f],
                 start=(g == 0),
                 stop=(g == NG - 1),
             )
 
-        load_x(0)
-        xsc = const.tile([P, 4], F32, name="xsc")
-        nc.scalar.dma_start(out=xsc[:], in_=x_scale.rearrange("o (p t) -> p (o t)", t=4))
-        nat = const.tile([P, GT], BF16, name="nat")
-        nc.vector.memset(nat[:], 0.0)
-        nc.scalar.dma_start(out=nat[0:NG, :], in_=s.rearrange("(g n) -> g n", n=GT))
-        nc.scalar.dma_start(out=nat[NG : 2 * NG, :], in_=wt.rearrange("(g n) -> g n", n=GT))
-        ident = const.tile([P, P], F32, name="ident")
-        make_identity(nc, ident[:])
-        a_raw = const.tile([P, 4, R], BF16, name="a_raw")
-        nc.sync.dma_start(out=a_raw[:], in_=a.rearrange("(p j) r -> p j r", j=4))
-        w_raw = const.tile([P, 4, F], BF16, name="w_raw")
-        wsrc = wm.rearrange("(p j) f -> p j f", j=4)
-        nc.sync.dma_start(out=w_raw[:, :, 0:512], in_=wsrc[:, :, 0:512])
-        load_t(0, 2)
-        nc.sync.dma_start(out=w_raw[:, :, 512:1024], in_=wsrc[:, :, 512:1024])
-        load_x(1)
-        load_x(2)
-        load_t(1, 1)
+        def flush_o(i):
+            for g in range(i):
+                if ("o", g) not in st and ("uq", g // UQ) in st and ("eq", g) in st:
+                    st["o", g] = True
+                    mm_o(g, 0)
+                    mm_o(g, 1)
 
-        warm = const.tile([P, 1], F32, name="warm")
-        nc.vector.memset(warm[:], 0.0)
-        nc.scalar.activation(out=warm[:], in_=warm[:], func=ACT.Tanh)
-        for t in range(4):
-            cast(0, t)
-        transposes(0, 0)
-        transposes(0, 1)
-        scale_x(0, 0)
-        scale_x(0, 1)
-        wi = const.tile([P, F, 4], BF16, name="wi", align_bytes=64)
-        ai = const.tile([P, R, 4], BF16, name="ai", align_bytes=64)
-        aq = const.tile([P, R], U32, name="aq", align_bytes=64)
-        as_ = const.tile([P, R], U8, name="as_", align_bytes=64)
-        wq = const.tile([P, F], U32, name="wq", align_bytes=64)
-        ws = const.tile([P, F], U8, name="ws", align_bytes=64)
-        nc.vector.tensor_copy(out=ai[:], in_=a_raw[:].rearrange("p j r -> p r j"))
-        quant_x(0)
-        natf = const.tile([P, GT], F32, name="natf")
-        nc.gpsimd.tensor_copy(out=natf[:], in_=nat[:])
-        nc.vector.tensor_copy(out=wi[:, 0:256, :], in_=w_raw[:, :, 0:256].rearrange("p j f -> p f j"))
-        nc.scalar.copy(out=wi[:, 256:512, :], in_=w_raw[:, :, 256:512].rearrange("p j f -> p f j"))
-        nc.vector.quantize_mx(out=aq[:].bitcast(FP8X4), scales=as_[:], in_=ai[:].rearrange("p r j -> p (r j)"))
-        sw_ps = ps_u.tile([P, 512], F32, name="ub")
-        for t in range(4):
-            nc.tensor.transpose(sw_ps[:, t * 128 : (t + 1) * 128], natf[:, t::4], ident[:])
-        sw = const.tile([P, 2 * NG, 4], F32, name="sw")
-        nc.vector.quantize_mx(out=wq[:, 0:256].bitcast(FP8X4), scales=ws[:, 0:256], in_=wi[:, 0:256, :].rearrange("p f j -> p (f j)"))
-        nc.vector.tensor_copy(out=sw[:], in_=sw_ps[:].rearrange("p (t n) -> p n t", t=4)[:, 0 : 2 * NG, :])
-        nc.vector.quantize_mx(out=wq[:, 256:512].bitcast(FP8X4), scales=ws[:, 256:512], in_=wi[:, 256:512, :].rearrange("p f j -> p (f j)"))
-        mm_u(0)
-        gate_u(0)
-        nc.vector.tensor_copy(out=wi[:, 512:768, :], in_=w_raw[:, :, 512:768].rearrange("p j f -> p f j"))
-        nc.scalar.copy(out=wi[:, 768:1024, :], in_=w_raw[:, :, 768:1024].rearrange("p j f -> p f j"))
-        quant_u(0)
-        acc = []
-        for h in range(2):
-            acc_t = ps_acc.tile([P, 512], F32, name="acc%d" % h)
-            acc.append(acc_t)
-        for t in range(4):
-            cast(1, t)
-        mm_y(0, 0)
-        mm_y(0, 1)
-        transposes(1, 0)
-        transposes(1, 1)
-
-        for i in range(NG):
-            for c in range(NC):
-                if c == 0:
-                    if i + 3 < NG:
-                        load_x(i + 3)
-                    if i + 2 < NG:
-                        load_t(i + 2, 1)
-                if c % 2 == 0 and i + 2 < NG:
-                    cast(i + 2, c // 2)
-                nxt = c + 2
-                if nxt < NC:
-                    mm_y(i, nxt)
-                elif i + 1 < NG:
-                    mm_y(i + 1, nxt - NC)
-                sub(i, c)
-                if i == 0 and c == 0:
-                    nc.vector.quantize_mx(out=wq[:, 512:768].bitcast(FP8X4), scales=ws[:, 512:768], in_=wi[:, 512:768, :].rearrange("p f j -> p (f j)"))
-                if i == 0 and c == 1:
-                    nc.vector.quantize_mx(out=wq[:, 768:1024].bitcast(FP8X4), scales=ws[:, 768:1024], in_=wi[:, 768:1024, :].rearrange("p f j -> p (f j)"))
-                tanh(i, c)
-                weight(i, c)
-                if c == 0 and i + 1 < NG:
-                    scale_x(i + 1, 0)
-                if c == 1 and i > 0:
-                    quant_e(i - 1, 1)
-                if c == 2:
-                    if i > 0:
-                        mm_o(i - 1, 0)
-                    if i + 1 < NG:
-                        scale_x(i + 1, 1)
-                if c == 3 and i > 0:
-                    mm_o(i - 1, 1)
-                if c == 4:
-                    if i + 1 < NG:
-                        quant_x(i + 1)
-                    if i + 2 < NG:
-                        transposes(i + 2, 0)
-                if c == 5 and i + 1 < NG:
-                    mm_u(i + 1)
-                if c == 6 and i + 1 < NG:
-                    gate_u(i + 1)
-                if c == 6 and i + 2 < NG:
-                    transposes(i + 2, 1)
-                if c == 7:
-                    quant_e(i, 0)
-                    if i + 1 < NG:
-                        quant_u(i + 1)
-
-        quant_e(NG - 1, 1)
-        for h in range(2):
-            mm_o(NG - 1, h)
+        def finish(h):
             res = work.tile([P, 512], F32, name="res")
             inv = 1.0 / math.sqrt(T)
             if h == 0:
@@ -293,3 +204,157 @@ def tile_lorafalogcoshgradient_t_kernel(tc, x_bytes, x_scale, wm, a, target, s, 
             else:
                 nc.vector.tensor_scalar(out=res[:], in0=acc[h][:], scalar1=inv, scalar2=None, op0=ALU.mult)
             nc.sync.dma_start(out=out[:, h * 512 : (h + 1) * 512], in_=res[:])
+
+        def w_inter(eng, lo):
+            eng(out=wi[:, lo : lo + 256, :], in_=w_raw[:, :, lo : lo + 256].rearrange("p j f -> p f j"))
+
+        def w_quant(lo):
+            nc.vector.quantize_mx(
+                out=wq[:, lo : lo + 256].bitcast(FP8X4),
+                scales=ws[:, lo : lo + 256],
+                in_=wi[:, lo : lo + 256, :].rearrange("p f j -> p (f j)"),
+            )
+
+        def g_inter(dst, src):
+            nc.gpsimd.tensor_scalar(out=dst, in0=src.rearrange("p j f -> p f j"), scalar1=1.0, scalar2=0.0, op0=ALU.mult, op1=ALU.add)
+
+        nat = const.tile([P, GT], BF16, name="nat")
+        nc.vector.memset(nat[:], 0.0)
+        ident = const.tile([P, P], F32, name="ident")
+        make_identity(nc, ident[:])
+        load_x(0)
+        nc.sync.dma_start(out=nat[0:NG, :], in_=s.rearrange("(g n) -> g n", n=GT))
+        nc.sync.dma_start(out=nat[NG : 2 * NG, :], in_=wt.rearrange("(g n) -> g n", n=GT))
+        w_raw = const.tile([P, 4, F], BF16, name="w_raw")
+        wsrc = wm.rearrange("(p j) f -> p j f", j=4)
+        nc.sync.dma_start(out=w_raw[:, :, 0:512], in_=wsrc[:, :, 0:512])
+        xsc = const.tile([P, 4], F32, name="xsc")
+        nc.sync.dma_start(out=xsc[:], in_=x_scale.rearrange("o (p t) -> p (o t)", t=4))
+        a_raw = const.tile([P, 4, R], BF16, name="a_raw")
+        load_t(0, 2)
+        nc.sync.dma_start(out=w_raw[:, :, 512:1024], in_=wsrc[:, :, 512:1024])
+        nc.sync.dma_start(out=a_raw[:], in_=a.rearrange("(p j) r -> p j r", j=4))
+        load_x(1)
+        load_x(2)
+        load_t(1, 1)
+
+        warm = const.tile([P, 1], F32, name="warm")
+        nc.vector.memset(warm[:], 0.0)
+        nc.scalar.activation(out=warm[:], in_=warm[:], func=ACT.Tanh)
+        natf = const.tile([P, GT], F32, name="natf")
+        sw = const.tile([P, 2 * NG, 4], F32, name="sw")
+        wi = const.tile([P, F, 4], BF16, name="wi", align_bytes=64)
+        ai = const.tile([P, R, 4], BF16, name="ai", align_bytes=64)
+        aq = const.tile([P, R], U32, name="aq", align_bytes=64)
+        as_ = const.tile([P, R], U8, name="as_", align_bytes=64)
+        wq = const.tile([P, F], U32, name="wq", align_bytes=64)
+        ws = const.tile([P, F], U8, name="ws", align_bytes=64)
+        acc = []
+        for h in range(2):
+            acc_t = ps_acc.tile([P, 512], F32, name="acc%d" % h)
+            acc.append(acc_t)
+
+        for t in range(4):
+            cast(0, t)
+        nc.vector.tensor_copy(out=natf[:], in_=nat[:])
+        sw_ps = ps_u.tile([P, 512], F32, name="ub")
+        for t in range(4):
+            nc.tensor.transpose(sw_ps[:, t * 128 : (t + 1) * 128], natf[:, t::4], ident[:])
+        w_inter(nc.vector.tensor_copy, 0)
+        transposes(0, 0)
+        transposes(0, 1)
+        w_inter(nc.scalar.copy, 256)
+        scale_x(0, 0)
+        scale_x(0, 1)
+        w_quant(0)
+        quant_x(0)
+        nc.vector.tensor_copy(out=sw[:], in_=sw_ps[:].rearrange("p (t n) -> p n t", t=4)[:, 0 : 2 * NG, :])
+        w_quant(256)
+        for t in range(4):
+            cast(1, t)
+        mm_y(0)
+        mm_y(1)
+        transposes(1, 0)
+        transposes(1, 1)
+        g_inter(wi[:, 512:768, :], w_raw[:, :, 512:768])
+        g_inter(wi[:, 768:1024, :], w_raw[:, :, 768:1024])
+        g_inter(ai[:], a_raw[:])
+
+        def slot0(c):
+            if c == 0:
+                w_quant(512)
+            elif c == 1:
+                w_quant(768)
+            elif c == 2:
+                nc.vector.quantize_mx(out=aq[:].bitcast(FP8X4), scales=as_[:], in_=ai[:].rearrange("p r j -> p (r j)"))
+                mm_u(0)
+            elif c == 3:
+                gate_u(0)
+
+        NS = NG * NC
+        done = set()
+        for n in range(NS + 4):
+            i, c = divmod(n, NC)
+            if n < NS:
+                if c == 0:
+                    if i + 3 < NG:
+                        load_x(i + 3)
+                    if i + 2 < NG:
+                        load_t(i + 2, 1)
+                sub(n)
+                if i == 0:
+                    slot0(c)
+                if n + 2 < NS:
+                    mm_y(n + 2)
+                tanh(n)
+            for m in range(max(0, n - 4), n + 1):
+                if m < NS and m not in done and m + LAG[engine_of(m)] <= n:
+                    done.add(m)
+                    weight(m)
+            if c == 0:
+                if i + 2 < NG:
+                    cast(i + 2, 0)
+                if i + 1 < NG:
+                    scale_x(i + 1, 0)
+            if c == 1:
+                if i + 2 < NG:
+                    cast(i + 2, 1)
+            if c == 2:
+                if i + 2 < NG:
+                    cast(i + 2, 2)
+                if i + 1 < NG:
+                    scale_x(i + 1, 1)
+            if c == 3:
+                if i + 2 < NG:
+                    cast(i + 2, 3)
+                if 0 < i < NG - 1:
+                    quant_e(i - 1, 0, F)
+            if i == NG - 1 and c == 5:
+                quant_e(i - 1, 0, F)
+                flush_o(i)
+            if c == 4:
+                if 0 < i < NG:
+                    flush_o(i)
+                if i + 2 < NG:
+                    transposes(i + 2, 0)
+            if c == 5:
+                if i + 1 < NG:
+                    quant_x(i + 1)
+            if c == 6:
+                if i + 1 < NG:
+                    mm_u(i + 1)
+                if i + 2 < NG:
+                    transposes(i + 2, 1)
+            if c == 7:
+                if i + 1 < NG:
+                    gate_u(i + 1)
+            if c == 1 and i % UQ == UQ - 1 and i < NG:
+                quant_u(i // UQ)
+
+            if n == NS - NC + 6:
+                quant_e(NG - 1, 0, 512)
+                mm_o(NG - 1, 0)
+                finish(0)
+        quant_e(NG - 1, 512, 1024)
+        mm_o(NG - 1, 1)
+        finish(1)

@@ -20,10 +20,14 @@ P = 128
 GT = 512
 NG = T // GT
 NC = F // 128
-MAPS = [["S","G","G","G","S","G","G","G"],["S","G","G","G","G","G","G","G"]]
-LAST = ["S","G","S","G","V","G","V","V"]
-LAG = {"G":0,"S":1,"V":2}
-UQ = 4
+MAPS = ["SSGGGGSG","SGGGGGGG"]
+LAST = "GGVVSVSV"
+SCHED = [["c01","G0","sx0"],["t1"],[],["G1","S1","sx1","c23"],["qx","t0","S1","qu"],["S1","mu","mo"],["G1","gu"],["G1","V0","qe"]]
+PLANES = 1
+RING, CODES, KEEP, XT, HS, REV = 5, 6, 4, 1, 0, 1
+TAIL = ["qeA","V1","G0","S0","fin0"]
+UQ = 2
+ZP = 2
 
 
 def tile_lorafalogcoshgradient_t_kernel(tc, x_bytes, x_scale, wm, a, target, s, wt, out):
@@ -32,13 +36,13 @@ def tile_lorafalogcoshgradient_t_kernel(tc, x_bytes, x_scale, wm, a, target, s, 
         const = ctx.enter_context(tc.tile_pool(name="const", bufs=1))
         load = ctx.enter_context(tc.tile_pool(name="load", bufs=4))
         work = ctx.enter_context(tc.tile_pool(name="work", bufs=2))
-        ring = ctx.enter_context(tc.tile_pool(name="ring", bufs=6))
-        keep = ctx.enter_context(tc.tile_pool(name="keep", bufs=3))
-        codes = ctx.enter_context(tc.tile_pool(name="codes", bufs=6))
+        ring = ctx.enter_context(tc.tile_pool(name="ring", bufs=RING))
+        keep = ctx.enter_context(tc.tile_pool(name="keep", bufs=KEEP))
+        codes = ctx.enter_context(tc.tile_pool(name="codes", bufs=CODES))
         ps_acc = ctx.enter_context(tc.psum_pool(name="ps_acc", bufs=1))
-        ps_xt = ctx.enter_context(tc.psum_pool(name="ps_xt", bufs=2))
+        ps_xt = ctx.enter_context(tc.psum_pool(name="ps_xt", bufs=XT))
         ps_u = ctx.enter_context(tc.psum_pool(name="ps_u", bufs=1))
-        ps_y = ctx.enter_context(tc.psum_pool(name="ps_y", bufs=3))
+        ps_y = ctx.enter_context(tc.psum_pool(name="ps_y", bufs=5 - XT))
         ctx.enter_context(tc.manual_schedule())
 
         st = {}
@@ -60,16 +64,20 @@ def tile_lorafalogcoshgradient_t_kernel(tc, x_bytes, x_scale, wm, a, target, s, 
             if t == 0:
                 st["xb", g] = work.tile([P, 4 * D], BF16, name="xb", align_bytes=64)
             nc.scalar.copy(out=st["xb", g][:, t * D : (t + n) * D], in_=st["xby", g][:, t * D : (t + n) * D].bitcast(FP8))
+            for k in range(t, t + n):
+                st["cast", g, k] = True
 
         def transposes(g, pair):
             xt = ps_xt.tile([P, 512], F32, name="xt")
             for tt in range(2):
+                assert st["cast", g, 2 * pair + tt]
                 words = st["xb", g][:, (2 * pair + tt) * D : (2 * pair + tt + 1) * D].bitcast(F32)
                 for u in range(2):
                     nc.tensor.transpose(xt[:, u * 256 + tt * 128 : u * 256 + (tt + 1) * 128], words[:, u::2], ident[:])
             st["xt", g, pair] = xt
 
         def scale_x(g, pair):
+            st["sx", g, pair] = True
             if pair == 0:
                 st["xi", g] = work.tile([P, 2048], BF16, name="xi", align_bytes=64)
             nc.vector.tensor_tensor(
@@ -80,6 +88,7 @@ def tile_lorafalogcoshgradient_t_kernel(tc, x_bytes, x_scale, wm, a, target, s, 
             )
 
         def quant_x(g):
+            assert st["sx", g, 0] and st["sx", g, 1]
             xq = work.tile([P, 512], U32, name="xq", align_bytes=64)
             xs = work.tile([P, 512], U8, name="xs", align_bytes=64)
             nc.vector.quantize_mx(out=xq[:].bitcast(FP8X4), scales=xs[:], in_=st["xi", g][:])
@@ -106,8 +115,18 @@ def tile_lorafalogcoshgradient_t_kernel(tc, x_bytes, x_scale, wm, a, target, s, 
 
         def gate_u(g):
             b, k = divmod(g, UQ)
+            st["gu", g] = True
             if k == 0:
                 st["ui", b] = work.tile([P, UQ * R, 4], BF16, name="ui", align_bytes=64)
+            if HS:
+                up = work.tile([P, 4, R], BF16, name="up", align_bytes=64)
+                for t in range(4):
+                    nc.scalar.activation(out=up[:, t, :], in_=st["ub", g][:, t * 128 : (t + 1) * 128], func=ACT.Copy, scale=sw[:, g, t : t + 1])
+                nc.scalar.copy(
+                    out=st["ui", b][:, k * R : (k + 1) * R, :].rearrange("p (c i) t -> p c t i", i=4),
+                    in_=up[:].rearrange("p t (c i) -> p c t i", i=4),
+                )
+                return
             nc.vector.tensor_tensor(
                 out=st["ui", b][:, k * R : (k + 1) * R, :],
                 in0=st["ub", g][:].rearrange("p (t r) -> p r t", t=4),
@@ -116,6 +135,8 @@ def tile_lorafalogcoshgradient_t_kernel(tc, x_bytes, x_scale, wm, a, target, s, 
             )
 
         def quant_u(b):
+            for k in range(UQ):
+                assert st["gu", b * UQ + k]
             uq = work.tile([P, UQ * R], U32, name="uq", align_bytes=64)
             us = work.tile([P, UQ * R], U8, name="us", align_bytes=64)
             nc.vector.quantize_mx(out=uq[:].bitcast(FP8X4), scales=us[:], in_=st["ui", b][:].rearrange("p r t -> p (r t)"))
@@ -129,42 +150,64 @@ def tile_lorafalogcoshgradient_t_kernel(tc, x_bytes, x_scale, wm, a, target, s, 
 
         def sub(n):
             g, c = divmod(n, NC)
-            z = ring.tile([P, 512], F32, name="z", align_bytes=64)
+            if ("z", n // ZP) not in st:
+                st["z", n // ZP] = ring.tile([P, 512 * ZP], F32, name="z", align_bytes=64)
+            z = st["z", n // ZP][:].rearrange("p (h n t) -> p h n t", h=2, t=2)[:, :, n % ZP * 128 : (n % ZP + 1) * 128, :]
             nc.vector.tensor_tensor(
-                out=z[:].rearrange("p (h n t) -> p h n t", h=2, t=2),
+                out=z,
                 in0=st["yb", n][:].rearrange("p (h t n) -> p h n t", h=2, t=2),
                 in1=st["tg", g][:, :, c * 128 : (c + 1) * 128].rearrange("p (h t) n -> p h n t", h=2),
                 op=ALU.subtract,
             )
-            st["z", n] = z
 
-        def tanh(n):
-            th = ring.tile([P, 128, 4], F32, name="th", align_bytes=64)
+        def tanh(m):
+            th = ring.tile([P, 128 * ZP, 4], F32, name="th", align_bytes=64)
             nc.scalar.activation(
                 out=th[:].rearrange("p n (h t) -> p n h t", h=2),
-                in_=st["z", n][:].rearrange("p (h n t) -> p n h t", h=2, t=2),
+                in_=st["z", m][:].rearrange("p (h n t) -> p n h t", h=2, t=2),
                 func=ACT.Tanh,
             )
-            st["th", n] = th
+            st["th", m] = th
 
-        def engine_of(n):
-            g, c = divmod(n, NC)
-            return LAST[c] if g == NG - 1 else MAPS[g % len(MAPS)][c]
+        NU = NC // ZP
 
-        def weight(n):
-            g, c = divmod(n, NC)
-            if ("e", g) not in st:
-                st["e", g] = keep.tile([P, F, 4], BF16, name="e", align_bytes=64)
-            dst = st["e", g][:, c * 128 : (c + 1) * 128, :]
-            th = st["th", n]
-            eng = engine_of(n)
-            if eng == "S":
-                for t in range(4):
-                    nc.scalar.activation(out=dst[:, :, t], in_=th[:, :, t], func=ACT.Copy, scale=sw[:, NG + g, t : t + 1])
+        pend = {"S": [], "G": [], "V": []}
+
+        def plan(m):
+            g, k = divmod(m, NU)
+            mp = (LAST if g == NG - 1 else MAPS[g % len(MAPS)])[k * 2 : k * 2 + 2]
+            if mp[0] == mp[1] and mp[0] in "SV":
+                pend[mp[0]].append((m, 0, 256))
             else:
-                (nc.gpsimd if eng == "G" else nc.vector).tensor_tensor(
-                    out=dst, in0=th[:], in1=sw[:, NG + g, :].unsqueeze(1).to_broadcast([P, 128, 4]), op=ALU.mult
-                )
+                pend[mp[0]].append((m, 0, 128))
+                pend[mp[1]].append((m, 128, 256))
+
+        def weigh(eng, upto):
+            while pend[eng] and pend[eng][0][0] <= upto:
+                m, lo, hi = pend[eng].pop(0)
+                g, k = divmod(m, NU)
+                if ("e", g) not in st:
+                    st["e", g] = keep.tile([P, F, 4], BF16, name="e", align_bytes=64)
+                dst = st["e", g][:, k * 256 + lo : k * 256 + hi, :]
+                th = st["th", m][:, lo:hi, :]
+                if eng == "S" and PLANES:
+                    ep = work.tile([P, 4, 256], BF16, name="ep", align_bytes=64)
+                    for t in range(4):
+                        nc.scalar.activation(out=ep[:, t, lo:hi], in_=th[:, :, t], func=ACT.Copy, scale=sw[:, NG + g, t : t + 1])
+                    nc.scalar.copy(
+                        out=dst.rearrange("p (c i) t -> p c t i", i=4), in_=ep[:, :, lo:hi].rearrange("p t (c i) -> p c t i", i=4)
+                    )
+                elif eng == "S":
+                    for t in range(4):
+                        nc.scalar.activation(out=dst[:, :, t], in_=th[:, :, t], func=ACT.Copy, scale=sw[:, NG + g, t : t + 1])
+                else:
+                    (nc.gpsimd if eng == "G" else nc.vector).tensor_tensor(
+                        out=dst, in0=th, in1=sw[:, NG + g, :].unsqueeze(1).to_broadcast([P, hi - lo, 4]), op=ALU.mult
+                    )
+
+        def weigh_all(upto):
+            for eng in "SGV":
+                weigh(eng, upto)
 
         def quant_e(g, lo, hi):
             if lo == 0:
@@ -223,16 +266,25 @@ def tile_lorafalogcoshgradient_t_kernel(tc, x_bytes, x_scale, wm, a, target, s, 
         ident = const.tile([P, P], F32, name="ident")
         make_identity(nc, ident[:])
         load_x(0)
-        nc.sync.dma_start(out=nat[0:NG, :], in_=s.rearrange("(g n) -> g n", n=GT))
-        nc.sync.dma_start(out=nat[NG : 2 * NG, :], in_=wt.rearrange("(g n) -> g n", n=GT))
         w_raw = const.tile([P, 4, F], BF16, name="w_raw")
         wsrc = wm.rearrange("(p j) f -> p j f", j=4)
-        nc.sync.dma_start(out=w_raw[:, :, 0:512], in_=wsrc[:, :, 0:512])
+
+        def load_w(lo, hi):
+            nc.sync.dma_start(out=w_raw[:, :, lo:hi], in_=wsrc[:, :, lo:hi])
+
+        load_w(0, 256)
         xsc = const.tile([P, 4], F32, name="xsc")
         nc.sync.dma_start(out=xsc[:], in_=x_scale.rearrange("o (p t) -> p (o t)", t=4))
+        load_w(256, 512)
+        nc.sync.dma_start(out=nat[0:NG, :], in_=s.rearrange("(g n) -> g n", n=GT))
+        nc.sync.dma_start(out=nat[NG : 2 * NG, :], in_=wt.rearrange("(g n) -> g n", n=GT))
         a_raw = const.tile([P, 4, R], BF16, name="a_raw")
-        load_t(0, 2)
-        nc.sync.dma_start(out=w_raw[:, :, 512:1024], in_=wsrc[:, :, 512:1024])
+        tg0 = load.tile([P, 4, F], BF16, name="tg", align_bytes=64)
+        tsrc0 = target[0:GT, :].rearrange("(p t) f -> p t f", t=4)
+        st["tg", 0] = tg0
+        nc.sync.dma_start(out=tg0[:, :, 0:512], in_=tsrc0[:, :, 0:512])
+        load_w(512, 1024)
+        nc.sync.dma_start(out=tg0[:, :, 512:1024], in_=tsrc0[:, :, 512:1024])
         nc.sync.dma_start(out=a_raw[:], in_=a.rearrange("(p j) r -> p j r", j=4))
         load_x(1)
         load_x(2)
@@ -256,26 +308,25 @@ def tile_lorafalogcoshgradient_t_kernel(tc, x_bytes, x_scale, wm, a, target, s, 
 
         for t in range(4):
             cast(0, t)
+        w_inter(nc.vector.tensor_copy, 0)
+        transposes(0, 0)
+        w_inter(nc.scalar.copy, 256)
+        scale_x(0, 0)
+        transposes(0, 1)
+        w_quant(0)
+        scale_x(0, 1)
         nc.vector.tensor_copy(out=natf[:], in_=nat[:])
         sw_ps = ps_u.tile([P, 512], F32, name="ub")
         for t in range(4):
             nc.tensor.transpose(sw_ps[:, t * 128 : (t + 1) * 128], natf[:, t::4], ident[:])
-        w_inter(nc.vector.tensor_copy, 0)
-        transposes(0, 0)
-        transposes(0, 1)
-        w_inter(nc.scalar.copy, 256)
-        scale_x(0, 0)
-        scale_x(0, 1)
-        w_quant(0)
         quant_x(0)
-        nc.vector.tensor_copy(out=sw[:], in_=sw_ps[:].rearrange("p (t n) -> p n t", t=4)[:, 0 : 2 * NG, :])
         w_quant(256)
+        nc.vector.tensor_copy(out=sw[:], in_=sw_ps[:].rearrange("p (t n) -> p n t", t=4)[:, 0 : 2 * NG, :])
         for t in range(4):
             cast(1, t)
         mm_y(0)
         mm_y(1)
         transposes(1, 0)
-        transposes(1, 1)
         g_inter(wi[:, 512:768, :], w_raw[:, :, 512:768])
         g_inter(wi[:, 768:1024, :], w_raw[:, :, 768:1024])
         g_inter(ai[:], a_raw[:])
@@ -292,69 +343,74 @@ def tile_lorafalogcoshgradient_t_kernel(tc, x_bytes, x_scale, wm, a, target, s, 
                 gate_u(0)
 
         NS = NG * NC
-        done = set()
-        for n in range(NS + 4):
-            i, c = divmod(n, NC)
-            if n < NS:
-                if c == 0:
-                    if i + 3 < NG:
-                        load_x(i + 3)
-                    if i + 2 < NG:
-                        load_t(i + 2, 1)
-                sub(n)
-                if i == 0:
-                    slot0(c)
-                if n + 2 < NS:
-                    mm_y(n + 2)
-                tanh(n)
-            for m in range(max(0, n - 4), n + 1):
-                if m < NS and m not in done and m + LAG[engine_of(m)] <= n:
-                    done.add(m)
-                    weight(m)
-            if c == 0:
-                if i + 2 < NG:
-                    cast(i + 2, 0)
-                if i + 1 < NG:
-                    scale_x(i + 1, 0)
-            if c == 1:
-                if i + 2 < NG:
-                    cast(i + 2, 1)
-            if c == 2:
-                if i + 2 < NG:
-                    cast(i + 2, 2)
-                if i + 1 < NG:
-                    scale_x(i + 1, 1)
-            if c == 3:
-                if i + 2 < NG:
-                    cast(i + 2, 3)
-                if 0 < i < NG - 1:
-                    quant_e(i - 1, 0, F)
-            if i == NG - 1 and c == 5:
-                quant_e(i - 1, 0, F)
-                flush_o(i)
-            if c == 4:
-                if 0 < i < NG:
-                    flush_o(i)
-                if i + 2 < NG:
-                    transposes(i + 2, 0)
-            if c == 5:
-                if i + 1 < NG:
-                    quant_x(i + 1)
-            if c == 6:
-                if i + 1 < NG:
-                    mm_u(i + 1)
-                if i + 2 < NG:
-                    transposes(i + 2, 1)
-            if c == 7:
-                if i + 1 < NG:
-                    gate_u(i + 1)
-            if c == 1 and i % UQ == UQ - 1 and i < NG:
-                quant_u(i // UQ)
 
-            if n == NS - NC + 6:
+        def run(names, m):
+            i = m // NU
+            for name in names:
+                k = name[0]
+                if k in "SGV":
+                    weigh(k, m - int(name[1]))
+                elif k == "c" and i + 2 < NG:
+                    cast(i + 2, int(name[1]), len(name) - 1)
+                elif name == "t0" and i + 2 < NG and XT == 1:
+                    transposes(i + 2, 0)
+                elif name == "t1" and i + 1 < NG and XT == 1:
+                    transposes(i + 1, 1)
+                elif name in ("sx0", "sx1") and i + 1 < NG:
+                    scale_x(i + 1, int(name[2]))
+                elif name == "qx" and i + 1 < NG:
+                    quant_x(i + 1)
+                elif name == "mu" and i + 1 < NG:
+                    mm_u(i + 1)
+                elif name == "gu" and i + 1 < NG:
+                    gate_u(i + 1)
+                elif name == "qu" and i % UQ == UQ - 1:
+                    quant_u(i // UQ)
+                elif name == "qu+" and i + 1 < NG and (i + 1) % UQ == UQ - 1:
+                    quant_u((i + 1) // UQ)
+                elif name == "qe" and i > 0:
+                    weigh_all((i - 1) * NU + NU - 1)
+                    quant_e(i - 1, 0, F)
+                elif name == "qe0" and i > 0:
+                    weigh_all((i - 1) * NU + 1)
+                    quant_e(i - 1, 0, 512)
+                elif name == "qe1" and i > 0:
+                    weigh_all((i - 1) * NU + 3)
+                    quant_e(i - 1, 512, 1024)
+                elif name == "mo":
+                    flush_o(i)
+
+        for m in range(NS // 2):
+            i, c = divmod(m, NU)
+            if c == 0:
+                if i + 3 < NG:
+                    load_x(i + 3)
+                if i + 2 < NG:
+                    load_t(i + 2, 1)
+            if 2 * m + 2 < NS:
+                mm_y(2 * m + 2)
+                mm_y(2 * m + 3)
+            sub(2 * m + REV)
+            if i == 0:
+                slot0(2 * c)
+            run(SCHED[2 * c], m)
+            sub(2 * m + 1 - REV)
+            if i == 0:
+                slot0(2 * c + 1)
+            tanh(m)
+            plan(m)
+            run(SCHED[2 * c + 1], m)
+        for name in TAIL:
+            if name == "qeA":
+                weigh_all(NS // 2 - 3)
                 quant_e(NG - 1, 0, 512)
+            elif name == "fin0":
+                flush_o(NG - 1)
                 mm_o(NG - 1, 0)
                 finish(0)
+            else:
+                weigh(name[0], NS // 2 - 1 - int(name[1]))
+        weigh_all(NS // 2 - 1)
         quant_e(NG - 1, 512, 1024)
         mm_o(NG - 1, 1)
         finish(1)

import math
from contextlib import ExitStack

import concourse.mybir as mybir
from concourse.masks import make_identity

T, D, F, R = 8192, 512, 1024, 128
FLOPS = 2 * T * D * (F + R) + 2 * T * R * F

F32 = mybir.dt.float32
BF16 = mybir.dt.bfloat16
U32 = mybir.dt.uint32
U8 = mybir.dt.uint8
FP8 = mybir.dt.float8_e4m3fn
FP8X4 = mybir.dt.float8_e4m3fn_x4
ACT = mybir.ActivationFunctionType
ALU = mybir.AluOpType

P = 128
GT = 512
NG = T // GT
NC = F // 128
MAPS = ["SSGGGGSG","SGGGGGGG"]
LAST = "GGVVSVSV"
SCHED = [["c01","G0","sx0"],["t1"],[],["G1","S1","sx1","c23"],["qx","t0","S1","qu"],["S1","mu","mo"],["G1","gu"],["G1","V0","qe"]]
PLANES = 1
RING, CODES, KEEP, XT, HS, REV = 5, 6, 4, 1, 0, 1
TAIL = ["qeA","V1","G0","S0","fin0"]
UQ = 2
ZP = 2


def tile_lorafalogcoshgradient_t_kernel(tc, x_bytes, x_scale, wm, a, target, s, wt, out):
    nc = tc.nc
    with ExitStack() as ctx:
        const = ctx.enter_context(tc.tile_pool(name="const", bufs=1))
        load = ctx.enter_context(tc.tile_pool(name="load", bufs=4))
        work = ctx.enter_context(tc.tile_pool(name="work", bufs=2))
        ring = ctx.enter_context(tc.tile_pool(name="ring", bufs=RING))
        keep = ctx.enter_context(tc.tile_pool(name="keep", bufs=KEEP))
        codes = ctx.enter_context(tc.tile_pool(name="codes", bufs=CODES))
        ps_acc = ctx.enter_context(tc.psum_pool(name="ps_acc", bufs=1))
        ps_xt = ctx.enter_context(tc.psum_pool(name="ps_xt", bufs=XT))
        ps_u = ctx.enter_context(tc.psum_pool(name="ps_u", bufs=1))
        ps_y = ctx.enter_context(tc.psum_pool(name="ps_y", bufs=5 - XT))
        ctx.enter_context(tc.manual_schedule())

        st = {}

        def load_x(g):
            xby = load.tile([P, 4 * D], U8, name="xby", align_bytes=64)
            nc.sync.dma_start(out=xby[:], in_=x_bytes[g * GT : (g + 1) * GT, :].rearrange("(p t) k -> p (t k)", t=4))
            st["xby", g] = xby

        def load_t(g, parts):
            tg = load.tile([P, 4, F], BF16, name="tg", align_bytes=64)
            src = target[g * GT : (g + 1) * GT, :].rearrange("(p t) f -> p t f", t=4)
            w = F // parts
            for i in range(parts):
                nc.sync.dma_start(out=tg[:, :, i * w : (i + 1) * w], in_=src[:, :, i * w : (i + 1) * w])
            st["tg", g] = tg

        def cast(g, t, n=1):
            if t == 0:
                st["xb", g] = work.tile([P, 4 * D], BF16, name="xb", align_bytes=64)
            nc.scalar.copy(out=st["xb", g][:, t * D : (t + n) * D], in_=st["xby", g][:, t * D : (t + n) * D].bitcast(FP8))
            for k in range(t, t + n):
                st["cast", g, k] = True

        def transposes(g, pair):
            xt = ps_xt.tile([P, 512], F32, name="xt")
            for tt in range(2):
                assert st["cast", g, 2 * pair + tt]
                words = st["xb", g][:, (2 * pair + tt) * D : (2 * pair + tt + 1) * D].bitcast(F32)
                for u in range(2):
                    nc.tensor.transpose(xt[:, u * 256 + tt * 128 : u * 256 + (tt + 1) * 128], words[:, u::2], ident[:])
            st["xt", g, pair] = xt

        def scale_x(g, pair):
            st["sx", g, pair] = True
            if pair == 0:
                st["xi", g] = work.tile([P, 2048], BF16, name="xi", align_bytes=64)
            nc.vector.tensor_tensor(
                out=st["xi", g][:, pair * 1024 : (pair + 1) * 1024].rearrange("p (n u e) -> p n u e", u=2, e=2),
                in0=st["xt", g, pair][:].bitcast(BF16).rearrange("p (u n e) -> p n u e", u=2, e=2),
                in1=xsc[:].rearrange("p (u e) -> p u e", e=2).unsqueeze(1).to_broadcast([P, 256, 2, 2]),
                op=ALU.mult,
            )

        def quant_x(g):
            assert st["sx", g, 0] and st["sx", g, 1]
            xq = work.tile([P, 512], U32, name="xq", align_bytes=64)
            xs = work.tile([P, 512], U8, name="xs", align_bytes=64)
            nc.vector.quantize_mx(out=xq[:].bitcast(FP8X4), scales=xs[:], in_=st["xi", g][:])
            st["xq", g] = (xq, xs)

        def mx4(bank, g, wq_, ws_, lo):
            xq, xs = st["xq", g]
            for t in range(4):
                c = slice(t * 128, (t + 1) * 128)
                nc.tensor.matmul_mx(
                    out=bank[:, c],
                    lhsT=xq[:, c].bitcast(FP8X4),
                    lhsT_scale=xs[:, c],
                    rhs=wq_[:, lo : lo + 128].bitcast(FP8X4),
                    rhs_scale=ws_[:, lo : lo + 128],
                    start=True,
                    stop=True,
                )

        def mm_u(g):
            ub = ps_u.tile([P, 512], F32, name="ub")
            mx4(ub, g, aq, as_, 0)
            st["ub", g] = ub

        def gate_u(g):
            b, k = divmod(g, UQ)
            st["gu", g] = True
            if k == 0:
                st["ui", b] = work.tile([P, UQ * R, 4], BF16, name="ui", align_bytes=64)
            if HS:
                up = work.tile([P, 4, R], BF16, name="up", align_bytes=64)
                for t in range(4):
                    nc.scalar.activation(out=up[:, t, :], in_=st["ub", g][:, t * 128 : (t + 1) * 128], func=ACT.Copy, scale=sw[:, g, t : t + 1])
                nc.scalar.copy(
                    out=st["ui", b][:, k * R : (k + 1) * R, :].rearrange("p (c i) t -> p c t i", i=4),
                    in_=up[:].rearrange("p t (c i) -> p c t i", i=4),
                )
                return
            nc.vector.tensor_tensor(
                out=st["ui", b][:, k * R : (k + 1) * R, :],
                in0=st["ub", g][:].rearrange("p (t r) -> p r t", t=4),
                in1=sw[:, g, :].unsqueeze(1).to_broadcast([P, R, 4]),
                op=ALU.mult,
            )

        def quant_u(b):
            for k in range(UQ):
                assert st["gu", b * UQ + k]
            uq = work.tile([P, UQ * R], U32, name="uq", align_bytes=64)
            us = work.tile([P, UQ * R], U8, name="us", align_bytes=64)
            nc.vector.quantize_mx(out=uq[:].bitcast(FP8X4), scales=us[:], in_=st["ui", b][:].rearrange("p r t -> p (r t)"))
            st["uq", b] = (uq, us)

        def mm_y(n):
            g, c = divmod(n, NC)
            yb = ps_y.tile([P, 512], F32, name="yb")
            mx4(yb, g, wq, ws, c * 128)
            st["yb", n] = yb

        def sub(n):
            g, c = divmod(n, NC)
            if ("z", n // ZP) not in st:
                st["z", n // ZP] = ring.tile([P, 512 * ZP], F32, name="z", align_bytes=64)
            z = st["z", n // ZP][:].rearrange("p (h n t) -> p h n t", h=2, t=2)[:, :, n % ZP * 128 : (n % ZP + 1) * 128, :]
            nc.vector.tensor_tensor(
                out=z,
                in0=st["yb", n][:].rearrange("p (h t n) -> p h n t", h=2, t=2),
                in1=st["tg", g][:, :, c * 128 : (c + 1) * 128].rearrange("p (h t) n -> p h n t", h=2),
                op=ALU.subtract,
            )

        def tanh(m):
            th = ring.tile([P, 128 * ZP, 4], F32, name="th", align_bytes=64)
            nc.scalar.activation(
                out=th[:].rearrange("p n (h t) -> p n h t", h=2),
                in_=st["z", m][:].rearrange("p (h n t) -> p n h t", h=2, t=2),
                func=ACT.Tanh,
            )
            st["th", m] = th

        NU = NC // ZP

        pend = {"S": [], "G": [], "V": []}

        def plan(m):
            g, k = divmod(m, NU)
            mp = (LAST if g == NG - 1 else MAPS[g % len(MAPS)])[k * 2 : k * 2 + 2]
            if mp[0] == mp[1] and mp[0] in "SV":
                pend[mp[0]].append((m, 0, 256))
            else:
                pend[mp[0]].append((m, 0, 128))
                pend[mp[1]].append((m, 128, 256))

        def weigh(eng, upto):
            while pend[eng] and pend[eng][0][0] <= upto:
                m, lo, hi = pend[eng].pop(0)
                g, k = divmod(m, NU)
                if ("e", g) not in st:
                    st["e", g] = keep.tile([P, F, 4], BF16, name="e", align_bytes=64)
                dst = st["e", g][:, k * 256 + lo : k * 256 + hi, :]
                th = st["th", m][:, lo:hi, :]
                if eng == "S" and PLANES:
                    ep = work.tile([P, 4, 256], BF16, name="ep", align_bytes=64)
                    for t in range(4):
                        nc.scalar.activation(out=ep[:, t, lo:hi], in_=th[:, :, t], func=ACT.Copy, scale=sw[:, NG + g, t : t + 1])
                    nc.scalar.copy(
                        out=dst.rearrange("p (c i) t -> p c t i", i=4), in_=ep[:, :, lo:hi].rearrange("p t (c i) -> p c t i", i=4)
                    )
                elif eng == "S":
                    for t in range(4):
                        nc.scalar.activation(out=dst[:, :, t], in_=th[:, :, t], func=ACT.Copy, scale=sw[:, NG + g, t : t + 1])
                else:
                    (nc.gpsimd if eng == "G" else nc.vector).tensor_tensor(
                        out=dst, in0=th, in1=sw[:, NG + g, :].unsqueeze(1).to_broadcast([P, hi - lo, 4]), op=ALU.mult
                    )

        def weigh_all(upto):
            for eng in "SGV":
                weigh(eng, upto)

        def quant_e(g, lo, hi):
            if lo == 0:
                st["eq", g] = (codes.tile([P, F], U32, name="eq", align_bytes=64), codes.tile([P, F], U8, name="es", align_bytes=64))
            eq, es = st["eq", g]
            nc.vector.quantize_mx(
                out=eq[:, lo:hi].bitcast(FP8X4), scales=es[:, lo:hi], in_=st["e", g][:, lo:hi, :].rearrange("p n t -> p (n t)")
            )

        def mm_o(g, h):
            uq, us = st["uq", g // UQ]
            eq, es = st["eq", g]
            k = slice(g % UQ * R, (g % UQ + 1) * R)
            f = slice(h * 512, (h + 1) * 512)
            nc.tensor.matmul_mx(
                out=acc[h][:],
                lhsT=uq[:, k].bitcast(FP8X4),
                lhsT_scale=us[:, k],
                rhs=eq[:, f].bitcast(FP8X4),
                rhs_scale=es[:, f],
                start=(g == 0),
                stop=(g == NG - 1),
            )

        def flush_o(i):
            for g in range(i):
                if ("o", g) not in st and ("uq", g // UQ) in st and ("eq", g) in st:
                    st["o", g] = True
                    mm_o(g, 0)
                    mm_o(g, 1)

        def finish(h):
            res = work.tile([P, 512], F32, name="res")
            inv = 1.0 / math.sqrt(T)
            if h == 0:
                nc.scalar.activation(out=res[:], in_=acc[h][:], func=ACT.Copy, scale=inv)
            else:
                nc.vector.tensor_scalar(out=res[:], in0=acc[h][:], scalar1=inv, scalar2=None, op0=ALU.mult)
            nc.sync.dma_start(out=out[:, h * 512 : (h + 1) * 512], in_=res[:])

        def w_inter(eng, lo):
            eng(out=wi[:, lo : lo + 256, :], in_=w_raw[:, :, lo : lo + 256].rearrange("p j f -> p f j"))

        def w_quant(lo):
            nc.vector.quantize_mx(
                out=wq[:, lo : lo + 256].bitcast(FP8X4),
                scales=ws[:, lo : lo + 256],
                in_=wi[:, lo : lo + 256, :].rearrange("p f j -> p (f j)"),
            )

        def g_inter(dst, src):
            nc.gpsimd.tensor_scalar(out=dst, in0=src.rearrange("p j f -> p f j"), scalar1=1.0, scalar2=0.0, op0=ALU.mult, op1=ALU.add)

        nat = const.tile([P, GT], BF16, name="nat")
        nc.vector.memset(nat[:], 0.0)
        ident = const.tile([P, P], F32, name="ident")
        make_identity(nc, ident[:])
        load_x(0)
        w_raw = const.tile([P, 4, F], BF16, name="w_raw")
        wsrc = wm.rearrange("(p j) f -> p j f", j=4)

        def load_w(lo, hi):
            nc.sync.dma_start(out=w_raw[:, :, lo:hi], in_=wsrc[:, :, lo:hi])

        load_w(0, 256)
        xsc = const.tile([P, 4], F32, name="xsc")
        nc.sync.dma_start(out=xsc[:], in_=x_scale.rearrange("o (p t) -> p (o t)", t=4))
        load_w(256, 512)
        nc.sync.dma_start(out=nat[0:NG, :], in_=s.rearrange("(g n) -> g n", n=GT))
        nc.sync.dma_start(out=nat[NG : 2 * NG, :], in_=wt.rearrange("(g n) -> g n", n=GT))
        a_raw = const.tile([P, 4, R], BF16, name="a_raw")
        tg0 = load.tile([P, 4, F], BF16, name="tg", align_bytes=64)
        tsrc0 = target[0:GT, :].rearrange("(p t) f -> p t f", t=4)
        st["tg", 0] = tg0
        nc.sync.dma_start(out=tg0[:, :, 0:512], in_=tsrc0[:, :, 0:512])
        load_w(512, 1024)
        nc.sync.dma_start(out=tg0[:, :, 512:1024], in_=tsrc0[:, :, 512:1024])
        nc.sync.dma_start(out=a_raw[:], in_=a.rearrange("(p j) r -> p j r", j=4))
        load_x(1)
        load_x(2)
        load_t(1, 1)

        warm = const.tile([P, 1], F32, name="warm")
        nc.vector.memset(warm[:], 0.0)
        nc.scalar.activation(out=warm[:], in_=warm[:], func=ACT.Tanh)
        natf = const.tile([P, GT], F32, name="natf")
        sw = const.tile([P, 2 * NG, 4], F32, name="sw")
        wi = const.tile([P, F, 4], BF16, name="wi", align_bytes=64)
        ai = const.tile([P, R, 4], BF16, name="ai", align_bytes=64)
        aq = const.tile([P, R], U32, name="aq", align_bytes=64)
        as_ = const.tile([P, R], U8, name="as_", align_bytes=64)
        wq = const.tile([P, F], U32, name="wq", align_bytes=64)
        ws = const.tile([P, F], U8, name="ws", align_bytes=64)
        acc = []
        for h in range(2):
            acc_t = ps_acc.tile([P, 512], F32, name="acc%d" % h)
            acc.append(acc_t)

        for t in range(4):
            cast(0, t)
        w_inter(nc.vector.tensor_copy, 0)
        transposes(0, 0)
        w_inter(nc.scalar.copy, 256)
        scale_x(0, 0)
        transposes(0, 1)
        w_quant(0)
        scale_x(0, 1)
        nc.vector.tensor_copy(out=natf[:], in_=nat[:])
        sw_ps = ps_u.tile([P, 512], F32, name="ub")
        for t in range(4):
            nc.tensor.transpose(sw_ps[:, t * 128 : (t + 1) * 128], natf[:, t::4], ident[:])
        quant_x(0)
        w_quant(256)
        nc.vector.tensor_copy(out=sw[:], in_=sw_ps[:].rearrange("p (t n) -> p n t", t=4)[:, 0 : 2 * NG, :])
        for t in range(4):
            cast(1, t)
        mm_y(0)
        mm_y(1)
        transposes(1, 0)
        g_inter(wi[:, 512:768, :], w_raw[:, :, 512:768])
        g_inter(wi[:, 768:1024, :], w_raw[:, :, 768:1024])
        g_inter(ai[:], a_raw[:])

        def slot0(c):
            if c == 0:
                w_quant(512)
            elif c == 1:
                w_quant(768)
            elif c == 2:
                nc.vector.quantize_mx(out=aq[:].bitcast(FP8X4), scales=as_[:], in_=ai[:].rearrange("p r j -> p (r j)"))
                mm_u(0)
            elif c == 3:
                gate_u(0)

        NS = NG * NC

        def run(names, m):
            i = m // NU
            for name in names:
                k = name[0]
                if k in "SGV":
                    weigh(k, m - int(name[1]))
                elif k == "c" and i + 2 < NG:
                    cast(i + 2, int(name[1]), len(name) - 1)
                elif name == "t0" and i + 2 < NG and XT == 1:
                    transposes(i + 2, 0)
                elif name == "t1" and i + 1 < NG and XT == 1:
                    transposes(i + 1, 1)
                elif name in ("sx0", "sx1") and i + 1 < NG:
                    scale_x(i + 1, int(name[2]))
                elif name == "qx" and i + 1 < NG:
                    quant_x(i + 1)
                elif name == "mu" and i + 1 < NG:
                    mm_u(i + 1)
                elif name == "gu" and i + 1 < NG:
                    gate_u(i + 1)
                elif name == "qu" and i % UQ == UQ - 1:
                    quant_u(i // UQ)
                elif name == "qu+" and i + 1 < NG and (i + 1) % UQ == UQ - 1:
                    quant_u((i + 1) // UQ)
                elif name == "qe" and i > 0:
                    weigh_all((i - 1) * NU + NU - 1)
                    quant_e(i - 1, 0, F)
                elif name == "qe0" and i > 0:
                    weigh_all((i - 1) * NU + 1)
                    quant_e(i - 1, 0, 512)
                elif name == "qe1" and i > 0:
                    weigh_all((i - 1) * NU + 3)
                    quant_e(i - 1, 512, 1024)
                elif name == "mo":
                    flush_o(i)

        for m in range(NS // 2):
            i, c = divmod(m, NU)
            if c == 0:
                if i + 3 < NG:
                    load_x(i + 3)
                if i + 2 < NG:
                    load_t(i + 2, 1)
            if 2 * m + 2 < NS:
                mm_y(2 * m + 2)
                mm_y(2 * m + 3)
            sub(2 * m + REV)
            if i == 0:
                slot0(2 * c)
            run(SCHED[2 * c], m)
            sub(2 * m + 1 - REV)
            if i == 0:
                slot0(2 * c + 1)
            tanh(m)
            plan(m)
            run(SCHED[2 * c + 1], m)
        for name in TAIL:
            if name == "qeA":
                weigh_all(NS // 2 - 3)
                quant_e(NG - 1, 0, 512)
            elif name == "fin0":
                flush_o(NG - 1)
                mm_o(NG - 1, 0)
                finish(0)
            else:
                weigh(name[0], NS // 2 - 1 - int(name[1]))
        weigh_all(NS // 2 - 1)
        quant_e(NG - 1, 512, 1024)
        mm_o(NG - 1, 1)
        finish(1)
